import numpy as np
import ml_dtypes


def mxq(x, axis, fmt="e4m3"):
    dtype, down = {"e4m3": (ml_dtypes.float8_e4m3fn, 7), "e5m2": (ml_dtypes.float8_e5m2, 14)}[fmt]
    v = np.moveaxis(np.asarray(x, np.float32).astype(ml_dtypes.bfloat16).astype(np.float64), axis, -1)
    blocks = v.reshape(v.shape[:-1] + (-1, 32))
    amax = np.abs(blocks).max(-1, keepdims=True)
    byte = np.maximum(np.where(amax > 0, np.frexp(amax)[1] - 1 + 127, 0) - down, 1)
    scale = np.exp2(byte - 127.0)
    codes = (blocks / scale).astype(np.float32).astype(dtype).astype(np.float64)
    return np.moveaxis((codes * scale).reshape(v.shape), -1, axis)


WIDE = False


def mx_kscale(k, group=512):
    if not WIDE:
        return np.ones(k)
    levels = np.array([10, -10, 5, -5, 0])
    if group != 512:
        return np.exp2(np.random.permutation(np.resize(levels, k // group))).repeat(group)
    if k % 512:
        return np.exp2(np.random.permutation(np.resize(levels, k // 32))).repeat(32)
    a = np.empty((k // 512, 16))
    for p in range(k // 512):
        a[p, :8] = np.random.permutation(np.resize(levels, 8))
        for g in range(8):
            far = levels[np.abs(levels - a[p, g]) >= 10]
            a[p, g + 8] = far[np.random.randint(len(far))]
    return np.exp2(a.ravel()).repeat(32)


def f64(x):
    return np.asarray(x).astype(np.float64)


E2M1 = np.array([0.0, 0.5, 1.0, 1.5, 2.0, 3.0, 4.0, 6.0, -0.0, -0.5, -1.0, -1.5, -2.0, -3.0, -4.0, -6.0])


def pack_group(w):
    k, n = w.shape
    w = f64(np.asarray(w, np.float32).astype(ml_dtypes.bfloat16)).reshape(k // 32, 32, n)
    amax = np.abs(w).max(1)
    mant, ex = np.frexp(amax / 6.0)
    byte = np.clip(np.where(amax > 0, np.where(mant > 0.5, ex, ex - 1) + 127, 1), 1, 254)
    scaled = (w * np.exp2(127.0 - byte)[:, None, :]).reshape(k, n).astype(np.float32)
    c = np.ascontiguousarray(scaled.reshape(k // 4, 4, n).transpose(0, 2, 1)).astype(ml_dtypes.float4_e2m1fn).view(np.uint8) & 0xF
    return np.ascontiguousarray((c[..., 0::2] | (c[..., 1::2] << 4)).reshape(k // 4, 2 * n)), byte.astype(np.uint8)


def unpack_group(words, scales):
    p, n = words.shape[0], scales.shape[1]
    words = np.ascontiguousarray(words).reshape(p, n, 2)
    nib = np.empty((p, n, 4), np.uint8)
    nib[..., 0::2] = words & 0xF
    nib[..., 1::2] = words >> 4
    return E2M1[nib].transpose(0, 2, 1).reshape(4 * p, n) * np.repeat(np.exp2(scales.astype(np.float64) - 127.0), 32, axis=0)


G, D, M, N = 2, 256, 256, 512


def setup_inputs():
    n = np.random.standard_normal
    s = mx_kscale(D, 0)[:, None]
    w_ = [pack_group(w) for w in n((G, D, M)) / np.sqrt(D) / s]
    u_ = [pack_group(w) for w in n((G, D, M)) / np.sqrt(D) / s]
    return {
        "x": (n((G, D, N)) * s).astype(np.float32),
        "w_words": np.stack([w[0] for w in w_]),
        "w_scales": np.stack([w[1] for w in w_]),
        "u_words": np.stack([w[0] for w in u_]),
        "u_scales": np.stack([w[1] for w in u_]),
        "r": n((G, M, N)).astype(np.float32),
    }


def reference(x, w_words, w_scales, u_words, u_scales, r):
    xq = mxq(f64(x), 1, "e4m3")
    h = np.stack([unpack_group(w_words[g], w_scales[g]) for g in range(G)]).transpose(0, 2, 1) @ xq
    g = np.stack([unpack_group(u_words[g], u_scales[g]) for g in range(G)]).transpose(0, 2, 1) @ xq
    y = np.tanh(h) * g
    y = y + f64(r)
    return y

@@ -1,0 +1,140 @@
+from contextlib import ExitStack
+
+import concourse.mybir as mybir
+
+G, D, M, N = 2, 256, 256, 512
+FLOPS = 2 * 2 * G * D * M * N
+
+F32 = mybir.dt.float32
+BF16 = mybir.dt.bfloat16
+I32 = mybir.dt.int32
+U32 = mybir.dt.uint32
+U8 = mybir.dt.uint8
+FP8X4 = mybir.dt.float8_e4m3fn_x4
+FP4X4 = mybir.dt.float4_e2m1fn_x4
+ALU = mybir.AluOpType
+TANH = mybir.ActivationFunctionType.Tanh
+
+P = 128
+PACK = 4
+ROWS = D // PACK
+QUAD = 32
+M_TILE = 128
+CHUNK = 256
+VEC_COLS = 160
+RUN = 4
+
+
+def tile_rows_gglu_tanh_res_kernel(tc, x, w_words, w_scales, u_words, u_scales, r, out):
+    nc = tc.nc
+    x_rows = x.rearrange("g (p j) n -> (g p) j n", j=PACK)
+    tiles = [(g, t) for t in range(M // M_TILE) for g in range(G)]
+
+    with ExitStack() as ctx:
+        sb = ctx.enter_context(tc.tile_pool(name="sb", bufs=1))
+        ps = ctx.enter_context(tc.psum_pool(name="ps", bufs=1))
+        ctx.enter_context(tc.manual_schedule())
+
+        raw = [sb.tile([P, PACK, CHUNK], F32, name="raw%d" % c, align_bytes=64) for c in range(N // CHUNK)]
+        grouped = [sb.tile([P, CHUNK, PACK], BF16, name="grouped%d" % c, align_bytes=64) for c in range(N // CHUNK)]
+        codes = sb.tile([P, N], U32, align_bytes=64)
+        x_plane = sb.tile([P, N], U8, align_bytes=64)
+        w_sb = sb.tile([P, 2 * M], U8, align_bytes=64)
+        u_sb = sb.tile([P, 2 * M], U8, align_bytes=64)
+        planes = sb.tile([P, 2 * M], U8, align_bytes=64)
+        r_sb = [sb.tile([P, G, N], F32, name="r%d" % t) for t in range(M // M_TILE)]
+
+        def load_x(c):
+            nc.sync.dma_start(out=raw[c][:], in_=x_rows[:, :, c * CHUNK : (c + 1) * CHUNK])
+
+        def load_words(dst, words):
+            nc.sync.dma_start(out=dst[:].bitcast(I32), in_=words.rearrange("g p b -> (g p) b").bitcast(I32))
+
+        def load_scales(which, scales, q):
+            rows = scales.rearrange("g f m -> (g f) m").bitcast(I32)
+            nc.sync.dma_start(
+                out=planes[QUAD * q : QUAD * q + 4, which * M : (which + 1) * M].bitcast(I32),
+                in_=rows[4 * q : 4 * q + 4, :],
+            )
+
+        def load_r(t):
+            nc.sync.dma_start(out=r_sb[t][:], in_=r[:, t * M_TILE : (t + 1) * M_TILE, :].rearrange("g p n -> p g n"))
+
+        nc.vector.memset(planes[:].bitcast(I32), 0)
+        load_x(0)
+        load_words(w_sb, w_words)
+        for q in range(4):
+            load_scales(0, w_scales, q)
+        load_scales(1, u_scales, 0)
+        load_x(1)
+        for q in range(1, 4):
+            load_scales(1, u_scales, q)
+        load_words(u_sb, u_words)
+        load_r(0)
+        load_r(1)
+
+        def interleave(copy, c, lo, hi):
+            copy(
+                out=grouped[c][:, lo:hi, :].rearrange("p (a i) j -> p a j i", i=RUN),
+                in_=raw[c][:, :, lo:hi].rearrange("p j (a i) -> p a j i", i=RUN),
+            )
+
+        for c in range(N // CHUNK):
+            interleave(nc.vector.tensor_copy, c, 0, VEC_COLS)
+            interleave(nc.scalar.copy, c, VEC_COLS, CHUNK)
+            cols = slice(c * CHUNK, (c + 1) * CHUNK)
+            nc.vector.quantize_mx(
+                out=codes[:, cols].bitcast(FP8X4),
+                scales=x_plane[:, cols],
+                in_=grouped[c][:].rearrange("p n j -> p (n j)"),
+            )
+
+        def product(acc, words_sb, which, g, t):
+            rows = slice(g * ROWS, (g + 1) * ROWS)
+            nc.tensor.matmul_mx(
+                out=acc[:],
+                lhsT=words_sb[rows, 2 * t * M_TILE : 2 * (t + 1) * M_TILE].bitcast(FP4X4),
+                lhsT_scale=planes[rows, which * M + t * M_TILE : which * M + (t + 1) * M_TILE],
+                rhs=codes[rows, :].bitcast(FP8X4),
+                rhs_scale=x_plane[rows, :],
+                start=True,
+                stop=True,
+            )
+
+        z = {}
+        gate = {}
+        for t in range(M // M_TILE):
+            for g in range(G):
+                z[g, t] = ps.tile([M_TILE, N], F32, name="z%d%d" % (g, t))
+                product(z[g, t], w_sb, 0, g, t)
+            for g in range(G):
+                gate[g, t] = ps.tile([M_TILE, N], F32, name="gate%d%d" % (g, t))
+                product(gate[g, t], u_sb, 1, g, t)
+
+        act = {}
+        y = {}
+        res = {}
+        for g, t in tiles:
+            act[g, t] = sb.tile([P, N], F32, name="act%d%d" % (g, t))
+            y[g, t] = sb.tile([P, N], F32, name="y%d%d" % (g, t))
+            res[g, t] = sb.tile([P, N], F32, name="res%d%d" % (g, t))
+            nc.scalar.activation(out=act[g, t][:], in_=z[g, t][:], func=TANH)
+
+        def multiply(key):
+            nc.vector.tensor_tensor(out=y[key][:], in0=gate[key][:], in1=act[key][:], op=ALU.mult)
+
+        def add(eng, key, lo, hi):
+            g, t = key
+            eng.tensor_tensor(out=res[key][:, lo:hi], in0=y[key][:, lo:hi], in1=r_sb[t][:, g, lo:hi], op=ALU.add)
+
+        def store(key, lo, hi):
+            g, t = key
+            nc.sync.dma_start(out=out[g, t * M_TILE : (t + 1) * M_TILE, lo:hi], in_=res[key][:, lo:hi])
+
+        multiply(tiles[0])
+        for i in range(1, len(tiles)):
+            multiply(tiles[i])
+            add(nc.vector, tiles[i - 1], 0, N)
+            store(tiles[i - 1], 0, N)
+        add(nc.vector, tiles[-1], 0, N)
+        store(tiles[-1], 0, N)

@@ -44,34 +44,34 @@ def tile_rows_gglu_tanh_res_kernel(tc, x, w_words, w_scales, u_words, u_scales, 
         planes = sb.tile([P, 2 * M], U8, align_bytes=64)
         r_sb = [sb.tile([P, G, N], F32, name="r%d" % t) for t in range(M // M_TILE)]
 
-        def load_x(c):
-            nc.sync.dma_start(out=raw[c][:], in_=x_rows[:, :, c * CHUNK : (c + 1) * CHUNK])
+        def load_x(queue, c):
+            queue.dma_start(out=raw[c][:], in_=x_rows[:, :, c * CHUNK : (c + 1) * CHUNK])
 
-        def load_words(dst, words):
-            nc.sync.dma_start(out=dst[:].bitcast(I32), in_=words.rearrange("g p b -> (g p) b").bitcast(I32))
+        def load_words(queue, dst, words):
+            queue.dma_start(out=dst[:].bitcast(I32), in_=words.rearrange("g p b -> (g p) b").bitcast(I32))
 
-        def load_scales(which, scales, q):
+        def load_scales(queue, which, scales, q):
             rows = scales.rearrange("g f m -> (g f) m").bitcast(I32)
-            nc.sync.dma_start(
+            queue.dma_start(
                 out=planes[QUAD * q : QUAD * q + 4, which * M : (which + 1) * M].bitcast(I32),
                 in_=rows[4 * q : 4 * q + 4, :],
             )
 
-        def load_r(t):
-            nc.sync.dma_start(out=r_sb[t][:], in_=r[:, t * M_TILE : (t + 1) * M_TILE, :].rearrange("g p n -> p g n"))
+        def load_r(queue, t):
+            queue.dma_start(out=r_sb[t][:], in_=r[:, t * M_TILE : (t + 1) * M_TILE, :].rearrange("g p n -> p g n"))
 
         nc.vector.memset(planes[:].bitcast(I32), 0)
-        load_x(0)
-        load_words(w_sb, w_words)
+        load_x(nc.sync, 0)
+        load_words(nc.sync, w_sb, w_words)
         for q in range(4):
-            load_scales(0, w_scales, q)
-        load_scales(1, u_scales, 0)
-        load_x(1)
+            load_scales(nc.sync, 0, w_scales, q)
+        load_scales(nc.sync, 1, u_scales, 0)
+        load_x(nc.sync, 1)
         for q in range(1, 4):
-            load_scales(1, u_scales, q)
-        load_words(u_sb, u_words)
-        load_r(0)
-        load_r(1)
+            load_scales(nc.sync, 1, u_scales, q)
+        load_words(nc.sync, u_sb, u_words)
+        load_r(nc.sync, 0)
+        load_r(nc.sync, 1)
 
         def interleave(copy, c, lo, hi):
             copy(
@@ -120,21 +120,32 @@ def tile_rows_gglu_tanh_res_kernel(tc, x, w_words, w_scales, u_words, u_scales, 
             res[g, t] = sb.tile([P, N], F32, name="res%d%d" % (g, t))
             nc.scalar.activation(out=act[g, t][:], in_=z[g, t][:], func=TANH)
 
-        def multiply(key):
-            nc.vector.tensor_tensor(out=y[key][:], in0=gate[key][:], in1=act[key][:], op=ALU.mult)
+        def multiply(key, lo, hi):
+            nc.vector.tensor_tensor(out=y[key][:, lo:hi], in0=gate[key][:, lo:hi], in1=act[key][:, lo:hi], op=ALU.mult)
 
         def add(eng, key, lo, hi):
             g, t = key
             eng.tensor_tensor(out=res[key][:, lo:hi], in0=y[key][:, lo:hi], in1=r_sb[t][:, g, lo:hi], op=ALU.add)
 
-        def store(key, lo, hi):
+        def store(queue, key, lo, hi):
             g, t = key
-            nc.sync.dma_start(out=out[g, t * M_TILE : (t + 1) * M_TILE, lo:hi], in_=res[key][:, lo:hi])
+            queue.dma_start(out=out[g, t * M_TILE : (t + 1) * M_TILE, lo:hi], in_=res[key][:, lo:hi])
 
-        multiply(tiles[0])
-        for i in range(1, len(tiles)):
-            multiply(tiles[i])
-            add(nc.vector, tiles[i - 1], 0, N)
-            store(tiles[i - 1], 0, N)
-        add(nc.vector, tiles[-1], 0, N)
-        store(tiles[-1], 0, N)
+        half = N // 2
+        multiply(tiles[0], 0, half)
+        multiply(tiles[0], half, N)
+        add(nc.gpsimd, tiles[0], 0, half)
+        add(nc.gpsimd, tiles[0], half, N)
+        store(nc.sync, tiles[0], 0, N)
+        multiply(tiles[1], 0, N)
+        add(nc.gpsimd, tiles[1], 0, half)
+        multiply(tiles[2], 0, N)
+        multiply(tiles[3], 0, N)
+        add(nc.vector, tiles[1], half, N)
+        store(nc.sync, tiles[1], 0, N)
+        add(nc.vector, tiles[2], 0, N)
+        store(nc.sync, tiles[2], 0, N)
+        add(nc.vector, tiles[3], 0, half)
+        store(nc.sync, tiles[3], 0, half)
+        add(nc.vector, tiles[3], half, N)
+        store(nc.sync, tiles[3], half, N)

@@ -63,11 +63,12 @@ def tile_rows_gglu_tanh_res_kernel(tc, x, w_words, w_scales, u_words, u_scales, 
         nc.vector.memset(planes[:].bitcast(I32), 0)
         load_x(nc.sync, 0)
         load_words(nc.sync, w_sb, w_words)
-        for q in range(4):
+        for q in range(2):
             load_scales(nc.sync, 0, w_scales, q)
-        load_scales(nc.sync, 1, u_scales, 0)
         load_x(nc.sync, 1)
-        for q in range(1, 4):
+        for q in range(2, 4):
+            load_scales(nc.sync, 0, w_scales, q)
+        for q in range(4):
             load_scales(nc.sync, 1, u_scales, q)
         load_words(nc.sync, u_sb, u_words)
         load_r(nc.sync, 0)
@@ -107,10 +108,10 @@ def tile_rows_gglu_tanh_res_kernel(tc, x, w_words, w_scales, u_words, u_scales, 
             for g in range(G):
                 z[g, t] = ps.tile([M_TILE, N], F32, name="z%d%d" % (g, t))
                 product(z[g, t], w_sb, 0, g, t)
-            for g in range(G):
                 gate[g, t] = ps.tile([M_TILE, N], F32, name="gate%d%d" % (g, t))
                 product(gate[g, t], u_sb, 1, g, t)
 
+        halves = [(0, N // 2), (N // 2, N)]
         act = {}
         y = {}
         res = {}
@@ -118,7 +119,8 @@ def tile_rows_gglu_tanh_res_kernel(tc, x, w_words, w_scales, u_words, u_scales, 
             act[g, t] = sb.tile([P, N], F32, name="act%d%d" % (g, t))
             y[g, t] = sb.tile([P, N], F32, name="y%d%d" % (g, t))
             res[g, t] = sb.tile([P, N], F32, name="res%d%d" % (g, t))
-            nc.scalar.activation(out=act[g, t][:], in_=z[g, t][:], func=TANH)
+            for lo, hi in halves:
+                nc.scalar.activation(out=act[g, t][:, lo:hi], in_=z[g, t][:, lo:hi], func=TANH)
 
         def multiply(key, lo, hi):
             nc.vector.tensor_tensor(out=y[key][:, lo:hi], in0=gate[key][:, lo:hi], in1=act[key][:, lo:hi], op=ALU.mult)
@@ -131,21 +133,12 @@ def tile_rows_gglu_tanh_res_kernel(tc, x, w_words, w_scales, u_words, u_scales, 
             g, t = key
             queue.dma_start(out=out[g, t * M_TILE : (t + 1) * M_TILE, lo:hi], in_=res[key][:, lo:hi])
 
-        half = N // 2
-        multiply(tiles[0], 0, half)
-        multiply(tiles[0], half, N)
-        add(nc.gpsimd, tiles[0], 0, half)
-        add(nc.gpsimd, tiles[0], half, N)
-        store(nc.sync, tiles[0], 0, N)
-        multiply(tiles[1], 0, N)
-        add(nc.gpsimd, tiles[1], 0, half)
-        multiply(tiles[2], 0, N)
-        multiply(tiles[3], 0, N)
-        add(nc.vector, tiles[1], half, N)
-        store(nc.sync, tiles[1], 0, N)
-        add(nc.vector, tiles[2], 0, N)
-        store(nc.sync, tiles[2], 0, N)
-        add(nc.vector, tiles[3], 0, half)
-        store(nc.sync, tiles[3], 0, half)
-        add(nc.vector, tiles[3], half, N)
-        store(nc.sync, tiles[3], half, N)
+        for i, key in enumerate(tiles):
+            for lo, hi in halves:
+                multiply(key, lo, hi)
+            for lo, hi in halves:
+                add(nc.gpsimd if i < 2 else nc.vector, key, lo, hi)
+                if key == tiles[-1]:
+                    store(nc.sync, key, lo, hi)
+            if key != tiles[-1]:
+                store(nc.sync, key, 0, N)

@@ -63,14 +63,13 @@ def tile_rows_gglu_tanh_res_kernel(tc, x, w_words, w_scales, u_words, u_scales, 
         nc.vector.memset(planes[:].bitcast(I32), 0)
         load_x(nc.sync, 0)
         load_words(nc.sync, w_sb, w_words)
-        for q in range(2):
+        for q in range(4):
             load_scales(nc.sync, 0, w_scales, q)
         load_x(nc.sync, 1)
-        for q in range(2, 4):
-            load_scales(nc.sync, 0, w_scales, q)
-        for q in range(4):
-            load_scales(nc.sync, 1, u_scales, q)
+        load_scales(nc.sync, 1, u_scales, 0)
         load_words(nc.sync, u_sb, u_words)
+        for q in range(1, 4):
+            load_scales(nc.sync, 1, u_scales, q)
         load_r(nc.sync, 0)
         load_r(nc.sync, 1)
 
@@ -137,7 +136,7 @@ def tile_rows_gglu_tanh_res_kernel(tc, x, w_words, w_scales, u_words, u_scales, 
             for lo, hi in halves:
                 multiply(key, lo, hi)
             for lo, hi in halves:
-                add(nc.gpsimd if i < 2 else nc.vector, key, lo, hi)
+                add(nc.gpsimd if i < 0 else nc.vector, key, lo, hi)
                 if key == tiles[-1]:
                     store(nc.sync, key, lo, hi)
             if key != tiles[-1]:

from contextlib import ExitStack

import concourse.mybir as mybir

G, D, M, N = 2, 256, 256, 512
FLOPS = 2 * 2 * G * D * M * N

F32 = mybir.dt.float32
BF16 = mybir.dt.bfloat16
I32 = mybir.dt.int32
U32 = mybir.dt.uint32
U8 = mybir.dt.uint8
FP8X4 = mybir.dt.float8_e4m3fn_x4
FP4X4 = mybir.dt.float4_e2m1fn_x4
ALU = mybir.AluOpType
TANH = mybir.ActivationFunctionType.Tanh

P = 128
PACK = 4
ROWS = D // PACK
QUAD = 32
M_TILE = 128
CHUNK = 256
VEC_COLS = 160
RUN = 4


def tile_rows_gglu_tanh_res_kernel(tc, x, w_words, w_scales, u_words, u_scales, r, out):
    nc = tc.nc
    x_rows = x.rearrange("g (p j) n -> (g p) j n", j=PACK)
    tiles = [(g, t) for t in range(M // M_TILE) for g in range(G)]

    with ExitStack() as ctx:
        sb = ctx.enter_context(tc.tile_pool(name="sb", bufs=1))
        ps = ctx.enter_context(tc.psum_pool(name="ps", bufs=1))
        ctx.enter_context(tc.manual_schedule())

        raw = [sb.tile([P, PACK, CHUNK], F32, name="raw%d" % c, align_bytes=64) for c in range(N // CHUNK)]
        grouped = [sb.tile([P, CHUNK, PACK], BF16, name="grouped%d" % c, align_bytes=64) for c in range(N // CHUNK)]
        codes = sb.tile([P, N], U32, align_bytes=64)
        x_plane = sb.tile([P, N], U8, align_bytes=64)
        w_sb = sb.tile([P, 2 * M], U8, align_bytes=64)
        u_sb = sb.tile([P, 2 * M], U8, align_bytes=64)
        planes = sb.tile([P, 2 * M], U8, align_bytes=64)
        r_sb = [sb.tile([P, G, N], F32, name="r%d" % t) for t in range(M // M_TILE)]

        def load_x(queue, c):
            queue.dma_start(out=raw[c][:], in_=x_rows[:, :, c * CHUNK : (c + 1) * CHUNK])

        def load_words(queue, dst, words):
            queue.dma_start(out=dst[:].bitcast(I32), in_=words.rearrange("g p b -> (g p) b").bitcast(I32))

        def load_scales(queue, which, scales, q):
            rows = scales.rearrange("g f m -> (g f) m").bitcast(I32)
            queue.dma_start(
                out=planes[QUAD * q : QUAD * q + 4, which * M : (which + 1) * M].bitcast(I32),
                in_=rows[4 * q : 4 * q + 4, :],
            )

        def load_r(queue, t):
            queue.dma_start(out=r_sb[t][:], in_=r[:, t * M_TILE : (t + 1) * M_TILE, :].rearrange("g p n -> p g n"))

        nc.vector.memset(planes[:].bitcast(I32), 0)
        load_x(nc.sync, 0)
        load_words(nc.sync, w_sb, w_words)
        for q in range(4):
            load_scales(nc.sync, 0, w_scales, q)
        load_x(nc.sync, 1)
        load_scales(nc.sync, 1, u_scales, 0)
        load_words(nc.sync, u_sb, u_words)
        for q in range(1, 4):
            load_scales(nc.sync, 1, u_scales, q)
        load_r(nc.sync, 0)
        load_r(nc.sync, 1)

        def interleave(copy, c, lo, hi):
            copy(
                out=grouped[c][:, lo:hi, :].rearrange("p (a i) j -> p a j i", i=RUN),
                in_=raw[c][:, :, lo:hi].rearrange("p j (a i) -> p a j i", i=RUN),
            )

        for c in range(N // CHUNK):
            interleave(nc.vector.tensor_copy, c, 0, VEC_COLS)
            interleave(nc.scalar.copy, c, VEC_COLS, CHUNK)
            cols = slice(c * CHUNK, (c + 1) * CHUNK)
            nc.vector.quantize_mx(
                out=codes[:, cols].bitcast(FP8X4),
                scales=x_plane[:, cols],
                in_=grouped[c][:].rearrange("p n j -> p (n j)"),
            )

        def product(acc, words_sb, which, g, t):
            rows = slice(g * ROWS, (g + 1) * ROWS)
            nc.tensor.matmul_mx(
                out=acc[:],
                lhsT=words_sb[rows, 2 * t * M_TILE : 2 * (t + 1) * M_TILE].bitcast(FP4X4),
                lhsT_scale=planes[rows, which * M + t * M_TILE : which * M + (t + 1) * M_TILE],
                rhs=codes[rows, :].bitcast(FP8X4),
                rhs_scale=x_plane[rows, :],
                start=True,
                stop=True,
            )

        z = {}
        gate = {}
        for t in range(M // M_TILE):
            for g in range(G):
                z[g, t] = ps.tile([M_TILE, N], F32, name="z%d%d" % (g, t))
                product(z[g, t], w_sb, 0, g, t)
                gate[g, t] = ps.tile([M_TILE, N], F32, name="gate%d%d" % (g, t))
                product(gate[g, t], u_sb, 1, g, t)

        halves = [(0, N // 2), (N // 2, N)]
        act = {}
        y = {}
        res = {}
        for g, t in tiles:
            act[g, t] = sb.tile([P, N], F32, name="act%d%d" % (g, t))
            y[g, t] = sb.tile([P, N], F32, name="y%d%d" % (g, t))
            res[g, t] = sb.tile([P, N], F32, name="res%d%d" % (g, t))
            for lo, hi in halves:
                nc.scalar.activation(out=act[g, t][:, lo:hi], in_=z[g, t][:, lo:hi], func=TANH)

        def multiply(key, lo, hi):
            nc.vector.tensor_tensor(out=y[key][:, lo:hi], in0=gate[key][:, lo:hi], in1=act[key][:, lo:hi], op=ALU.mult)

        def add(eng, key, lo, hi):
            g, t = key
            eng.tensor_tensor(out=res[key][:, lo:hi], in0=y[key][:, lo:hi], in1=r_sb[t][:, g, lo:hi], op=ALU.add)

        def store(queue, key, lo, hi):
            g, t = key
            queue.dma_start(out=out[g, t * M_TILE : (t + 1) * M_TILE, lo:hi], in_=res[key][:, lo:hi])

        for i, key in enumerate(tiles):
            for lo, hi in halves:
                multiply(key, lo, hi)
            for lo, hi in halves:
                add(nc.gpsimd if i < 0 else nc.vector, key, lo, hi)
                if key == tiles[-1]:
                    store(nc.sync, key, lo, hi)
            if key != tiles[-1]:
                store(nc.sync, key, 0, N)
